import numpy as np
import ml_dtypes


def mxq(x, axis, fmt="e4m3"):
    dtype, down = {"e4m3": (ml_dtypes.float8_e4m3fn, 7), "e5m2": (ml_dtypes.float8_e5m2, 14)}[fmt]
    v = np.moveaxis(np.asarray(x, np.float32).astype(ml_dtypes.bfloat16).astype(np.float64), axis, -1)
    blocks = v.reshape(v.shape[:-1] + (-1, 32))
    amax = np.abs(blocks).max(-1, keepdims=True)
    byte = np.maximum(np.where(amax > 0, np.frexp(amax)[1] - 1 + 127, 0) - down, 1)
    scale = np.exp2(byte - 127.0)
    codes = (blocks / scale).astype(np.float32).astype(dtype).astype(np.float64)
    return np.moveaxis((codes * scale).reshape(v.shape), -1, axis)


WIDE = False


def mx_kscale(k):
    if not WIDE:
        return np.ones(k)
    levels = np.array([30, -30])
    if k % 512:
        return np.exp2(np.random.permutation(np.resize(levels, k // 32))).repeat(32)
    a = np.empty((k // 512, 16))
    for p in range(k // 512):
        a[p, :8] = np.random.permutation(np.resize(levels, 8))
        for g in range(8):
            far = levels[np.abs(levels - a[p, g]) >= 10]
            a[p, g + 8] = far[np.random.randint(len(far))]
    return np.exp2(a.ravel()).repeat(32)


def f64(x):
    return np.asarray(x).astype(np.float64)


def striped(idx):
    return np.tile(np.asarray(idx).reshape(-1, 16).T, (8, 1)).astype(np.uint16)


def unstriped(offs):
    return offs[:16].T.reshape(-1).astype(np.int64)


E2M1 = np.array([0.0, 0.5, 1.0, 1.5, 2.0, 3.0, 4.0, 6.0, -0.0, -0.5, -1.0, -1.5, -2.0, -3.0, -4.0, -6.0])


def pack_weight(w, fmt):
    k, n = w.shape
    w = f64(np.asarray(w, np.float32).astype(ml_dtypes.bfloat16)).reshape(k // 32, 32, n)
    amax = np.abs(w).max(1)
    if fmt == "e4m3":
        byte = np.frexp(amax)[1] - 1 + 127 - 7
    else:
        mant, ex = np.frexp(amax / 6.0)
        byte = np.where(mant > 0.5, ex, ex - 1) + 127
    byte = np.clip(np.where(amax > 0, byte, 1), 1, 254)
    scaled = (w * np.exp2(127.0 - byte)[:, None, :]).reshape(k, n).astype(np.float32)
    by_word = np.ascontiguousarray(scaled.reshape(k // 512, 128, 4, n).transpose(0, 1, 3, 2))
    if fmt == "e4m3":
        words = by_word.astype(ml_dtypes.float8_e4m3fn).view(np.uint8)
    else:
        c = by_word.astype(ml_dtypes.float4_e2m1fn).view(np.uint8) & 0xF
        words = (c[..., 0::2] | (c[..., 1::2] << 4)).reshape(k // 512, 128, 2 * n)
    return np.ascontiguousarray(words), np.ascontiguousarray(byte.astype(np.uint8).reshape(k // 512, 16, n))


def unpack_weight(words, scales, fmt):
    g, _, n = scales.shape
    words = np.ascontiguousarray(words).reshape(g, 128, n, -1)
    if fmt == "e4m3":
        vals = words.view(ml_dtypes.float8_e4m3fn).astype(np.float64)
    else:
        nib = np.empty((g, 128, n, 4), np.uint8)
        nib[..., 0::2] = words & 0xF
        nib[..., 1::2] = words >> 4
        vals = E2M1[nib]
    vals = vals * np.repeat(np.exp2(scales.astype(np.float64) - 127.0), 8, axis=1)[..., None]
    return vals.transpose(0, 1, 3, 2).reshape(g * 512, n)


def sigmoid(v):
    return 1.0 / (1.0 + np.exp(-v))


def sgn(shape):
    return np.random.uniform(0.5, 2.0, shape) * np.where(np.random.standard_normal(shape) < 0, -1.0, 1.0)


K, T, J, R, O, N, E = 512, 1024, 256, 512, 128, 256, 1024


def setup_inputs():
    n = np.random.standard_normal
    idx = np.random.permutation(T)[:J]
    idx2 = np.random.permutation(J)[:O]
    idx3 = np.random.permutation(J)[:O]
    idx4 = np.random.permutation(J)[:O]
    idx5 = np.random.permutation(J)[:O]
    idx6 = np.random.permutation(T)[:O]
    idx7 = np.random.permutation(E)[:O]
    fk = mx_kscale(K)
    fr = mx_kscale(R)
    xtp = pack_weight(n((K, T)) / fk[:, None], "e2m1")
    wp = pack_weight(n((K, R)) * 1 / np.sqrt(K) * fk[:, None], "e4m3")
    wbp = pack_weight(n((R, N)) * 1 / np.sqrt(R) / fr[:, None], "e2m1")
    wsp = pack_weight(n((K, N)) * 1 / np.sqrt(K) * fk[:, None], "e4m3")
    return {
        "xt_words": xtp[0],
        "xt_scales": xtp[1],
        "w_words": wp[0],
        "w_scales": wp[1],
        "sa": (np.random.uniform(0.5, 1.6, (R, 1)) * fr[:, None]).astype(np.float32),
        "sb": (np.random.uniform(0.5, 1.6, (R, 1)) * fr[:, None]).astype(np.float32),
        "sg": (sgn((R, 1))).astype(np.float32),
        "bg": (np.random.uniform(-2.0, 2.0, (R, 1))).astype(np.float32),
        "sh": (sgn((R, 1))).astype(np.float32),
        "bh": (np.random.uniform(-2.0, 2.0, (R, 1))).astype(np.float32),
        "wb_words": wbp[0],
        "wb_scales": wbp[1],
        "ws_words": wsp[0],
        "ws_scales": wsp[1],
        "offs": striped(idx),
        "offs2": striped(idx2),
        "offs3": striped(idx3),
        "offs4": striped(idx4),
        "offs5": striped(idx5),
        "offs6": striped(idx6),
        "offs7": striped(idx7),
    }


def reference(xt_words, xt_scales, w_words, w_scales, sa, sb, sg, bg, sh, bh, wb_words, wb_scales, ws_words, ws_scales, offs, offs2, offs3, offs4, offs5, offs6, offs7):
    idx = unstriped(offs)
    idx2 = unstriped(offs2)
    idx3 = unstriped(offs3)
    idx4 = unstriped(offs4)
    idx5 = unstriped(offs5)
    idx6 = unstriped(offs6)
    idx7 = unstriped(offs7)
    xtu = unpack_weight(xt_words, xt_scales, "e2m1")
    wu = unpack_weight(w_words, w_scales, "e4m3")
    wbu = unpack_weight(wb_words, wb_scales, "e2m1")
    wsu = unpack_weight(ws_words, ws_scales, "e4m3")
    xtidxg = xtu[:, idx]
    a = wu.T @ xtidxg
    u1 = a[:, idx2] * f64(sa) * sigmoid(a[:, idx3] * f64(sg) + f64(bg))
    u2 = a[:, idx4] * f64(sb) * sigmoid(a[:, idx5] * f64(sh) + f64(bh))
    hid = np.maximum(u1, u2)
    hidq = mxq(hid, 0, "e5m2")
    xtidx6g = xtu[:, idx6]
    p = wbu.T @ hidq + wsu.T @ xtidx6g
    y = np.zeros((N, E))
    y[:, idx7] = p
    return y

@@ -1,0 +1,192 @@
+from contextlib import ExitStack
+
+import concourse.mybir as mybir
+
+K, T, J, R, O, N, E = 512, 1024, 256, 512, 128, 256, 1024
+FLOPS = 2 * (K * R * J + R * N * O + K * N * O)
+
+F32 = mybir.dt.float32
+BF16 = mybir.dt.bfloat16
+I32 = mybir.dt.int32
+U32 = mybir.dt.uint32
+U16 = mybir.dt.uint16
+U8 = mybir.dt.uint8
+E4M3 = mybir.dt.float8_e4m3fn_x4
+E5M2 = mybir.dt.float8_e5m2_x4
+E2M1 = mybir.dt.float4_e2m1fn_x4
+ACT = mybir.ActivationFunctionType
+ALU = mybir.AluOpType
+
+P = 128
+PACK = 4
+QUAD = 32
+
+
+def tile_list_gatedtwins_solo_further_scattered_kernel(
+    tc, xt_words, xt_scales, w_words, w_scales, sa, sb, sg, bg, sh, bh,
+    wb_words, wb_scales, ws_words, ws_scales,
+    offs, offs2, offs3, offs4, offs5, offs6, offs7, out,
+):
+    nc = tc.nc
+    with ExitStack() as ctx:
+        keep = ctx.enter_context(tc.tile_pool(name="keep", bufs=1))
+        psum = ctx.enter_context(tc.psum_pool(name="psum", bufs=1))
+
+        def sbuf(name, shape, dtype):
+            return keep.tile(shape, dtype, name=name, align_bytes=64)
+
+        def load_list(name, src):
+            tile = sbuf(name, list(src.shape), U16)
+            nc.sync.dma_start(tile[:], src)
+            return tile
+
+        def load_rowwise(name, src):
+            tile = sbuf(name, [P, PACK], F32)
+            nc.sync.dma_start(tile[:], src.rearrange("(p t) o -> p (t o)", t=PACK))
+            return tile
+
+        def zeroed_plane(name, cols):
+            tile = sbuf(name, [P, cols], U8)
+            nc.vector.memset(tile[:].bitcast(I32), 0)
+            return tile
+
+        def load_scale_row(queue, plane, src, r):
+            rows = src[0].rearrange("(q r) c -> r q c", r=PACK)
+            queue.dma_start(plane[r:P:QUAD, :].bitcast(I32), rows[r].bitcast(I32))
+
+        xs_all = zeroed_plane("xs_all", T)
+        wsc_spread = zeroed_plane("wsc_spread", R)
+
+        list1 = load_list("list1", offs)
+        wsc_rows = sbuf("wsc_rows", [PACK, PACK, R // 4], I32)
+        nc.scalar.dma_start(wsc_rows[:], w_scales[0].rearrange("(q r) c -> r q c", r=PACK).bitcast(I32))
+        xw_all = sbuf("xw_all", [P, T], U16)
+        nc.sync.dma_start(xw_all[:].bitcast(I32), xt_words[0].bitcast(I32))
+        ww_all = sbuf("ww_all", [P, R], I32)
+        nc.sync.dma_start(ww_all[:], w_words[0].rearrange("p c t -> p (c t)").bitcast(I32))
+        for r in range(PACK):
+            load_scale_row(nc.sync if r % 2 == 0 else nc.scalar, xs_all, xt_scales, r)
+
+        list3 = load_list("list3", offs3)
+        sg_t = load_rowwise("sg_t", sg)
+        bg_t = load_rowwise("bg_t", bg)
+        list2 = load_list("list2", offs2)
+        sa_t = load_rowwise("sa_t", sa)
+        list5 = load_list("list5", offs5)
+        sh_t = load_rowwise("sh_t", sh)
+        bh_t = load_rowwise("bh_t", bh)
+        list4 = load_list("list4", offs4)
+        sb_t = load_rowwise("sb_t", sb)
+
+        ws_plane = zeroed_plane("ws_plane", N)
+        wb_plane = zeroed_plane("wb_plane", N)
+        pages = [sbuf("page%d" % h, [P, E], F32) for h in range(N // P)]
+        for page in pages:
+            nc.vector.memset(page[:], 0.0)
+
+        list6 = load_list("list6", offs6)
+        ws_w = sbuf("ws_w", [P, N], I32)
+        nc.sync.dma_start(ws_w[:], ws_words[0].rearrange("p c t -> p (c t)").bitcast(I32))
+        for r in range(PACK):
+            load_scale_row(nc.sync, ws_plane, ws_scales, r)
+        wb_w = sbuf("wb_w", [P, N], U16)
+        nc.sync.dma_start(wb_w[:].bitcast(I32), wb_words[0].bitcast(I32))
+        for r in range(PACK):
+            load_scale_row(nc.sync, wb_plane, wb_scales, r)
+        list7 = load_list("list7", offs7)
+
+        for q in range(PACK):
+            nc.vector.tensor_copy(wsc_spread[QUAD * q : QUAD * q + PACK, :].bitcast(I32), wsc_rows[:, q, :])
+        xw1 = sbuf("xw1", [P, J], U16)
+        nc.vector.tensor_copy(xw1[:], xw_all[:].indirect(list1[:]))
+        wsc_by_t = wsc_spread[:].rearrange("p (m t) -> p t m", t=PACK)
+        wsc_first = sbuf("wsc_first", [P, P], U8)
+        nc.vector.tensor_copy(wsc_first[:], wsc_by_t[:, 0, :])
+        xs1 = sbuf("xs1", [P, J], U8)
+        nc.vector.tensor_copy(xs1[:], xs_all[:].indirect(list1[:]))
+        wsc_rest = sbuf("wsc_rest", [P, PACK - 1, P], U8)
+        nc.vector.tensor_copy(wsc_rest[:], wsc_by_t[:, 1:PACK, :])
+
+        ww_mt = ww_all[:].bitcast(U32).rearrange("p (m t) -> p m t", t=PACK)
+        ww_first = sbuf("ww_first", [P, P], U32)
+        nc.scalar.copy(ww_first[:], ww_mt[:, :, 0])
+        ww_rest = sbuf("ww_rest", [P, PACK - 1, P], U32)
+        nc.scalar.copy(ww_rest[:].rearrange("p t m -> p m t"), ww_mt[:, :, 1:PACK])
+
+        a_tiles = []
+        for t in range(PACK):
+            bank = psum.tile([P, J], F32, name="a_bank%d" % t)
+            nc.tensor.matmul_mx(
+                bank[:],
+                lhsT=(ww_first[:] if t == 0 else ww_rest[:, t - 1, :]).bitcast(E4M3),
+                lhsT_scale=wsc_first[:] if t == 0 else wsc_rest[:, t - 1, :],
+                rhs=xw1[:].bitcast(E2M1),
+                rhs_scale=xs1[:],
+                start=True,
+                stop=True,
+            )
+            a_t = sbuf("a%d" % t, [P, J], F32)
+            nc.vector.tensor_copy(a_t[:], bank[:])
+            a_tiles.append(a_t)
+
+        hid = sbuf("hid", [P, O, PACK], BF16)
+
+        def gated(name, t, gate_list, slope, offset, value_list, weight):
+            gate = sbuf("gate_%s%d" % (name, t), [P, O], F32)
+            nc.scalar.activation(
+                gate[:], a_tiles[t][:].indirect(gate_list[:]), ACT.Sigmoid,
+                bias=offset[:, t : t + 1], scale=slope[:, t : t + 1],
+            )
+            value = sbuf("value_%s%d" % (name, t), [P, O], F32)
+            nc.scalar.activation(
+                value[:], a_tiles[t][:].indirect(value_list[:]), ACT.Copy, scale=weight[:, t : t + 1],
+            )
+            u = sbuf("u_%s%d" % (name, t), [P, O], F32)
+            nc.vector.tensor_tensor(u[:], value[:], gate[:], ALU.mult)
+            return u
+
+        def first_twin(t):
+            return gated("one", t, list3, sg_t, bg_t, list2, sa_t)
+
+        def second_twin_and_max(t, u1):
+            u2 = gated("two", t, list5, sh_t, bh_t, list4, sb_t)
+            nc.vector.tensor_tensor(hid[:, :, t], u1[:], u2[:], ALU.max)
+
+        u1_0 = first_twin(0)
+        u1_1 = first_twin(1)
+        second_twin_and_max(0, u1_0)
+        second_twin_and_max(1, u1_1)
+
+        xw6 = sbuf("xw6", [P, O], U16)
+        nc.vector.tensor_copy(xw6[:], xw_all[:].indirect(list6[:]))
+        xs6 = sbuf("xs6", [P, O], U8)
+        nc.vector.tensor_copy(xs6[:], xs_all[:].indirect(list6[:]))
+        p_banks = [psum.tile([P, O], F32, name="p_bank%d" % h) for h in range(N // P)]
+        for h in range(N // P):
+            cols = slice(h * P, (h + 1) * P)
+            nc.tensor.matmul_mx(
+                p_banks[h][:], lhsT=ws_w[:, cols].bitcast(E4M3), lhsT_scale=ws_plane[:, cols],
+                rhs=xw6[:].bitcast(E2M1), rhs_scale=xs6[:], start=True, stop=False,
+            )
+
+        for t in range(2, PACK):
+            second_twin_and_max(t, first_twin(t))
+
+        hid_codes = sbuf("hid_codes", [P, O], U32)
+        hid_scales = sbuf("hid_scales", [P, O], U8)
+        nc.vector.quantize_mx(hid_codes[:].bitcast(E5M2), hid_scales[:], hid[:].rearrange("p o t -> p (o t)"))
+        for h in range(N // P):
+            cols = slice(h * P, (h + 1) * P)
+            nc.tensor.matmul_mx(
+                p_banks[h][:], lhsT=wb_w[:, cols].bitcast(E2M1), lhsT_scale=wb_plane[:, cols],
+                rhs=hid_codes[:].bitcast(E5M2), rhs_scale=hid_scales[:], start=False, stop=True,
+            )
+
+        p0 = sbuf("p0", [P, O], F32)
+        nc.vector.tensor_copy(p0[:], p_banks[0][:])
+        nc.vector.tensor_copy(pages[0][:].indirect(list7[:]), p0[:])
+        nc.sync.dma_start(out[0:P, :], pages[0][:])
+        p1 = sbuf("p1", [P, O], F32)
+        nc.scalar.copy(p1[:], p_banks[1][:])
+        nc.scalar.activation(pages[1][:].indirect(list7[:]), p1[:], ACT.Copy)
+        nc.scalar.dma_start(out[P : 2 * P, :], pages[1][:])

@@ -59,19 +59,25 @@ def tile_list_gatedtwins_solo_further_scattered_kernel(
 
         list1 = load_list("list1", offs)
         wsc_rows = sbuf("wsc_rows", [PACK, PACK, R // 4], I32)
-        nc.scalar.dma_start(wsc_rows[:], w_scales[0].rearrange("(q r) c -> r q c", r=PACK).bitcast(I32))
+        nc.sync.dma_start(wsc_rows[:], w_scales[0].rearrange("(q r) c -> r q c", r=PACK).bitcast(I32))
         xw_all = sbuf("xw_all", [P, T], U16)
         nc.sync.dma_start(xw_all[:].bitcast(I32), xt_words[0].bitcast(I32))
         ww_all = sbuf("ww_all", [P, R], I32)
         nc.sync.dma_start(ww_all[:], w_words[0].rearrange("p c t -> p (c t)").bitcast(I32))
         for r in range(PACK):
-            load_scale_row(nc.sync if r % 2 == 0 else nc.scalar, xs_all, xt_scales, r)
+            load_scale_row(nc.scalar, xs_all, xt_scales, r)
+
+        warm_in = sbuf("warm_in", [P, 1], F32)
+        nc.vector.memset(warm_in[:], 0.0)
+        warm_out = sbuf("warm_out", [P, 1], F32)
+        nc.scalar.activation(warm_out[:], warm_in[:], ACT.Sigmoid)
 
         list3 = load_list("list3", offs3)
         sg_t = load_rowwise("sg_t", sg)
         bg_t = load_rowwise("bg_t", bg)
         list2 = load_list("list2", offs2)
         sa_t = load_rowwise("sa_t", sa)
+        list6 = load_list("list6", offs6)
         list5 = load_list("list5", offs5)
         sh_t = load_rowwise("sh_t", sh)
         bh_t = load_rowwise("bh_t", bh)
@@ -80,11 +86,7 @@ def tile_list_gatedtwins_solo_further_scattered_kernel(
 
         ws_plane = zeroed_plane("ws_plane", N)
         wb_plane = zeroed_plane("wb_plane", N)
-        pages = [sbuf("page%d" % h, [P, E], F32) for h in range(N // P)]
-        for page in pages:
-            nc.vector.memset(page[:], 0.0)
 
-        list6 = load_list("list6", offs6)
         ws_w = sbuf("ws_w", [P, N], I32)
         nc.sync.dma_start(ws_w[:], ws_words[0].rearrange("p c t -> p (c t)").bitcast(I32))
         for r in range(PACK):
@@ -98,14 +100,17 @@ def tile_list_gatedtwins_solo_further_scattered_kernel(
         for q in range(PACK):
             nc.vector.tensor_copy(wsc_spread[QUAD * q : QUAD * q + PACK, :].bitcast(I32), wsc_rows[:, q, :])
         xw1 = sbuf("xw1", [P, J], U16)
-        nc.vector.tensor_copy(xw1[:], xw_all[:].indirect(list1[:]))
         wsc_by_t = wsc_spread[:].rearrange("p (m t) -> p t m", t=PACK)
         wsc_first = sbuf("wsc_first", [P, P], U8)
-        nc.vector.tensor_copy(wsc_first[:], wsc_by_t[:, 0, :])
+        nc.gpsimd.tensor_copy(wsc_first[:], wsc_by_t[:, 0, :])
         xs1 = sbuf("xs1", [P, J], U8)
-        nc.vector.tensor_copy(xs1[:], xs_all[:].indirect(list1[:]))
+        for half in range(2):
+            slots = slice(half * P, (half + 1) * P)
+            entries = list1[:, half * (P // 16) : (half + 1) * (P // 16)]
+            nc.vector.tensor_copy(xw1[:, slots], xw_all[:].indirect(entries))
+            nc.vector.tensor_copy(xs1[:, slots], xs_all[:].indirect(entries))
         wsc_rest = sbuf("wsc_rest", [P, PACK - 1, P], U8)
-        nc.vector.tensor_copy(wsc_rest[:], wsc_by_t[:, 1:PACK, :])
+        nc.gpsimd.tensor_copy(wsc_rest[:], wsc_by_t[:, 1:PACK, :])
 
         ww_mt = ww_all[:].bitcast(U32).rearrange("p (m t) -> p m t", t=PACK)
         ww_first = sbuf("ww_first", [P, P], U32)
@@ -113,49 +118,49 @@ def tile_list_gatedtwins_solo_further_scattered_kernel(
         ww_rest = sbuf("ww_rest", [P, PACK - 1, P], U32)
         nc.scalar.copy(ww_rest[:].rearrange("p t m -> p m t"), ww_mt[:, :, 1:PACK])
 
+        pages = [sbuf(name, [P, E], F32) for name in ("ww_all", "wsc_spread")]
+        for page in pages:
+            nc.gpsimd.memset(page[:], 0.0)
+
         a_tiles = []
         for t in range(PACK):
-            bank = psum.tile([P, J], F32, name="a_bank%d" % t)
-            nc.tensor.matmul_mx(
-                bank[:],
-                lhsT=(ww_first[:] if t == 0 else ww_rest[:, t - 1, :]).bitcast(E4M3),
-                lhsT_scale=wsc_first[:] if t == 0 else wsc_rest[:, t - 1, :],
-                rhs=xw1[:].bitcast(E2M1),
-                rhs_scale=xs1[:],
-                start=True,
-                stop=True,
-            )
             a_t = sbuf("a%d" % t, [P, J], F32)
-            nc.vector.tensor_copy(a_t[:], bank[:])
+            width = P if t == 0 else J
+            for j0 in range(0, J, width):
+                slots = slice(j0, j0 + width)
+                bank = psum.tile([P, width], F32, name="a_bank%d_%d" % (t, j0))
+                nc.tensor.matmul_mx(
+                    bank[:],
+                    lhsT=(ww_first[:] if t == 0 else ww_rest[:, t - 1, :]).bitcast(E4M3),
+                    lhsT_scale=wsc_first[:] if t == 0 else wsc_rest[:, t - 1, :],
+                    rhs=xw1[:, slots].bitcast(E2M1),
+                    rhs_scale=xs1[:, slots],
+                    start=True,
+                    stop=True,
+                )
+                nc.vector.tensor_copy(a_t[:, slots], bank[:])
             a_tiles.append(a_t)
 
-        hid = sbuf("hid", [P, O, PACK], BF16)
-
-        def gated(name, t, gate_list, slope, offset, value_list, weight):
+        def gated(name, t, u, gate_list, slope, offset, value_list, weight):
             gate = sbuf("gate_%s%d" % (name, t), [P, O], F32)
             nc.scalar.activation(
                 gate[:], a_tiles[t][:].indirect(gate_list[:]), ACT.Sigmoid,
                 bias=offset[:, t : t + 1], scale=slope[:, t : t + 1],
             )
             value = sbuf("value_%s%d" % (name, t), [P, O], F32)
-            nc.scalar.activation(
-                value[:], a_tiles[t][:].indirect(value_list[:]), ACT.Copy, scale=weight[:, t : t + 1],
-            )
-            u = sbuf("u_%s%d" % (name, t), [P, O], F32)
-            nc.vector.tensor_tensor(u[:], value[:], gate[:], ALU.mult)
-            return u
+            width = O // 2 if (name, t) == ("two", PACK - 1) else O
+            for o0 in range(0, O, width):
+                places = slice(o0, o0 + width)
+                entries = value_list[:, o0 // 16 : (o0 + width) // 16]
+                nc.scalar.activation(
+                    value[:, places], a_tiles[t][:].indirect(entries), ACT.Copy, scale=weight[:, t : t + 1],
+                )
+                nc.vector.tensor_tensor(u[:, t, places], value[:, places], gate[:, places], ALU.mult)
 
-        def first_twin(t):
-            return gated("one", t, list3, sg_t, bg_t, list2, sa_t)
-
-        def second_twin_and_max(t, u1):
-            u2 = gated("two", t, list5, sh_t, bh_t, list4, sb_t)
-            nc.vector.tensor_tensor(hid[:, :, t], u1[:], u2[:], ALU.max)
-
-        u1_0 = first_twin(0)
-        u1_1 = first_twin(1)
-        second_twin_and_max(0, u1_0)
-        second_twin_and_max(1, u1_1)
+        u1 = sbuf("u1", [P, PACK, O], F32)
+        u2 = sbuf("u2", [P, PACK, O], F32)
+        for t in range(PACK):
+            gated("one", t, u1, list3, sg_t, bg_t, list2, sa_t)
 
         xw6 = sbuf("xw6", [P, O], U16)
         nc.vector.tensor_copy(xw6[:], xw_all[:].indirect(list6[:]))
@@ -169,12 +174,25 @@ def tile_list_gatedtwins_solo_further_scattered_kernel(
                 rhs=xw6[:].bitcast(E2M1), rhs_scale=xs6[:], start=True, stop=False,
             )
 
-        for t in range(2, PACK):
-            second_twin_and_max(t, first_twin(t))
+        for t in range(PACK):
+            gated("two", t, u2, list5, sh_t, bh_t, list4, sb_t)
 
+        hid = sbuf("hid", [P, O, PACK], BF16)
         hid_codes = sbuf("hid_codes", [P, O], U32)
         hid_scales = sbuf("hid_scales", [P, O], U8)
-        nc.vector.quantize_mx(hid_codes[:].bitcast(E5M2), hid_scales[:], hid[:].rearrange("p o t -> p (o t)"))
+        halves = [slice(0, O // 2), slice(O // 2, O)]
+        for places in halves:
+            nc.vector.tensor_tensor(
+                hid[:, places, :].rearrange("p (c i) t -> p c t i", i=4),
+                u1[:, :, places].rearrange("p t (c i) -> p c t i", i=4),
+                u2[:, :, places].rearrange("p t (c i) -> p c t i", i=4),
+                ALU.max,
+            )
+        for places in halves:
+            nc.vector.quantize_mx(
+                hid_codes[:, places].bitcast(E5M2), hid_scales[:, places],
+                hid[:, places, :].rearrange("p o t -> p (o t)"),
+            )
         for h in range(N // P):
             cols = slice(h * P, (h + 1) * P)
             nc.tensor.matmul_mx(

from contextlib import ExitStack

import concourse.mybir as mybir

K, T, J, R, O, N, E = 512, 1024, 256, 512, 128, 256, 1024
FLOPS = 2 * (K * R * J + R * N * O + K * N * O)

F32 = mybir.dt.float32
BF16 = mybir.dt.bfloat16
I32 = mybir.dt.int32
U32 = mybir.dt.uint32
U16 = mybir.dt.uint16
U8 = mybir.dt.uint8
E4M3 = mybir.dt.float8_e4m3fn_x4
E5M2 = mybir.dt.float8_e5m2_x4
E2M1 = mybir.dt.float4_e2m1fn_x4
ACT = mybir.ActivationFunctionType
ALU = mybir.AluOpType

P = 128
PACK = 4
QUAD = 32


def tile_list_gatedtwins_solo_further_scattered_kernel(
    tc, xt_words, xt_scales, w_words, w_scales, sa, sb, sg, bg, sh, bh,
    wb_words, wb_scales, ws_words, ws_scales,
    offs, offs2, offs3, offs4, offs5, offs6, offs7, out,
):
    nc = tc.nc
    with ExitStack() as ctx:
        keep = ctx.enter_context(tc.tile_pool(name="keep", bufs=1))
        psum = ctx.enter_context(tc.psum_pool(name="psum", bufs=1))

        def sbuf(name, shape, dtype):
            return keep.tile(shape, dtype, name=name, align_bytes=64)

        def load_list(name, src):
            tile = sbuf(name, list(src.shape), U16)
            nc.sync.dma_start(tile[:], src)
            return tile

        def load_rowwise(name, src):
            tile = sbuf(name, [P, PACK], F32)
            nc.sync.dma_start(tile[:], src.rearrange("(p t) o -> p (t o)", t=PACK))
            return tile

        def zeroed_plane(name, cols):
            tile = sbuf(name, [P, cols], U8)
            nc.vector.memset(tile[:].bitcast(I32), 0)
            return tile

        def load_scale_row(queue, plane, src, r):
            rows = src[0].rearrange("(q r) c -> r q c", r=PACK)
            queue.dma_start(plane[r:P:QUAD, :].bitcast(I32), rows[r].bitcast(I32))

        xs_all = zeroed_plane("xs_all", T)
        wsc_spread = zeroed_plane("wsc_spread", R)

        list1 = load_list("list1", offs)
        wsc_rows = sbuf("wsc_rows", [PACK, PACK, R // 4], I32)
        nc.sync.dma_start(wsc_rows[:], w_scales[0].rearrange("(q r) c -> r q c", r=PACK).bitcast(I32))
        xw_all = sbuf("xw_all", [P, T], U16)
        nc.sync.dma_start(xw_all[:].bitcast(I32), xt_words[0].bitcast(I32))
        ww_all = sbuf("ww_all", [P, R], I32)
        nc.sync.dma_start(ww_all[:], w_words[0].rearrange("p c t -> p (c t)").bitcast(I32))
        for r in range(PACK):
            load_scale_row(nc.scalar, xs_all, xt_scales, r)

        warm_in = sbuf("warm_in", [P, 1], F32)
        nc.vector.memset(warm_in[:], 0.0)
        warm_out = sbuf("warm_out", [P, 1], F32)
        nc.scalar.activation(warm_out[:], warm_in[:], ACT.Sigmoid)

        list3 = load_list("list3", offs3)
        sg_t = load_rowwise("sg_t", sg)
        bg_t = load_rowwise("bg_t", bg)
        list2 = load_list("list2", offs2)
        sa_t = load_rowwise("sa_t", sa)
        list6 = load_list("list6", offs6)
        list5 = load_list("list5", offs5)
        sh_t = load_rowwise("sh_t", sh)
        bh_t = load_rowwise("bh_t", bh)
        list4 = load_list("list4", offs4)
        sb_t = load_rowwise("sb_t", sb)

        ws_plane = zeroed_plane("ws_plane", N)
        wb_plane = zeroed_plane("wb_plane", N)

        ws_w = sbuf("ws_w", [P, N], I32)
        nc.sync.dma_start(ws_w[:], ws_words[0].rearrange("p c t -> p (c t)").bitcast(I32))
        for r in range(PACK):
            load_scale_row(nc.sync, ws_plane, ws_scales, r)
        wb_w = sbuf("wb_w", [P, N], U16)
        nc.sync.dma_start(wb_w[:].bitcast(I32), wb_words[0].bitcast(I32))
        for r in range(PACK):
            load_scale_row(nc.sync, wb_plane, wb_scales, r)
        list7 = load_list("list7", offs7)

        for q in range(PACK):
            nc.vector.tensor_copy(wsc_spread[QUAD * q : QUAD * q + PACK, :].bitcast(I32), wsc_rows[:, q, :])
        xw1 = sbuf("xw1", [P, J], U16)
        wsc_by_t = wsc_spread[:].rearrange("p (m t) -> p t m", t=PACK)
        wsc_first = sbuf("wsc_first", [P, P], U8)
        nc.gpsimd.tensor_copy(wsc_first[:], wsc_by_t[:, 0, :])
        xs1 = sbuf("xs1", [P, J], U8)
        for half in range(2):
            slots = slice(half * P, (half + 1) * P)
            entries = list1[:, half * (P // 16) : (half + 1) * (P // 16)]
            nc.vector.tensor_copy(xw1[:, slots], xw_all[:].indirect(entries))
            nc.vector.tensor_copy(xs1[:, slots], xs_all[:].indirect(entries))
        wsc_rest = sbuf("wsc_rest", [P, PACK - 1, P], U8)
        nc.gpsimd.tensor_copy(wsc_rest[:], wsc_by_t[:, 1:PACK, :])

        ww_mt = ww_all[:].bitcast(U32).rearrange("p (m t) -> p m t", t=PACK)
        ww_first = sbuf("ww_first", [P, P], U32)
        nc.scalar.copy(ww_first[:], ww_mt[:, :, 0])
        ww_rest = sbuf("ww_rest", [P, PACK - 1, P], U32)
        nc.scalar.copy(ww_rest[:].rearrange("p t m -> p m t"), ww_mt[:, :, 1:PACK])

        pages = [sbuf(name, [P, E], F32) for name in ("ww_all", "wsc_spread")]
        for page in pages:
            nc.gpsimd.memset(page[:], 0.0)

        a_tiles = []
        for t in range(PACK):
            a_t = sbuf("a%d" % t, [P, J], F32)
            width = P if t == 0 else J
            for j0 in range(0, J, width):
                slots = slice(j0, j0 + width)
                bank = psum.tile([P, width], F32, name="a_bank%d_%d" % (t, j0))
                nc.tensor.matmul_mx(
                    bank[:],
                    lhsT=(ww_first[:] if t == 0 else ww_rest[:, t - 1, :]).bitcast(E4M3),
                    lhsT_scale=wsc_first[:] if t == 0 else wsc_rest[:, t - 1, :],
                    rhs=xw1[:, slots].bitcast(E2M1),
                    rhs_scale=xs1[:, slots],
                    start=True,
                    stop=True,
                )
                nc.vector.tensor_copy(a_t[:, slots], bank[:])
            a_tiles.append(a_t)

        def gated(name, t, u, gate_list, slope, offset, value_list, weight):
            gate = sbuf("gate_%s%d" % (name, t), [P, O], F32)
            nc.scalar.activation(
                gate[:], a_tiles[t][:].indirect(gate_list[:]), ACT.Sigmoid,
                bias=offset[:, t : t + 1], scale=slope[:, t : t + 1],
            )
            value = sbuf("value_%s%d" % (name, t), [P, O], F32)
            width = O // 2 if (name, t) == ("two", PACK - 1) else O
            for o0 in range(0, O, width):
                places = slice(o0, o0 + width)
                entries = value_list[:, o0 // 16 : (o0 + width) // 16]
                nc.scalar.activation(
                    value[:, places], a_tiles[t][:].indirect(entries), ACT.Copy, scale=weight[:, t : t + 1],
                )
                nc.vector.tensor_tensor(u[:, t, places], value[:, places], gate[:, places], ALU.mult)

        u1 = sbuf("u1", [P, PACK, O], F32)
        u2 = sbuf("u2", [P, PACK, O], F32)
        for t in range(PACK):
            gated("one", t, u1, list3, sg_t, bg_t, list2, sa_t)

        xw6 = sbuf("xw6", [P, O], U16)
        nc.vector.tensor_copy(xw6[:], xw_all[:].indirect(list6[:]))
        xs6 = sbuf("xs6", [P, O], U8)
        nc.vector.tensor_copy(xs6[:], xs_all[:].indirect(list6[:]))
        p_banks = [psum.tile([P, O], F32, name="p_bank%d" % h) for h in range(N // P)]
        for h in range(N // P):
            cols = slice(h * P, (h + 1) * P)
            nc.tensor.matmul_mx(
                p_banks[h][:], lhsT=ws_w[:, cols].bitcast(E4M3), lhsT_scale=ws_plane[:, cols],
                rhs=xw6[:].bitcast(E2M1), rhs_scale=xs6[:], start=True, stop=False,
            )

        for t in range(PACK):
            gated("two", t, u2, list5, sh_t, bh_t, list4, sb_t)

        hid = sbuf("hid", [P, O, PACK], BF16)
        hid_codes = sbuf("hid_codes", [P, O], U32)
        hid_scales = sbuf("hid_scales", [P, O], U8)
        halves = [slice(0, O // 2), slice(O // 2, O)]
        for places in halves:
            nc.vector.tensor_tensor(
                hid[:, places, :].rearrange("p (c i) t -> p c t i", i=4),
                u1[:, :, places].rearrange("p t (c i) -> p c t i", i=4),
                u2[:, :, places].rearrange("p t (c i) -> p c t i", i=4),
                ALU.max,
            )
        for places in halves:
            nc.vector.quantize_mx(
                hid_codes[:, places].bitcast(E5M2), hid_scales[:, places],
                hid[:, places, :].rearrange("p o t -> p (o t)"),
            )
        for h in range(N // P):
            cols = slice(h * P, (h + 1) * P)
            nc.tensor.matmul_mx(
                p_banks[h][:], lhsT=wb_w[:, cols].bitcast(E2M1), lhsT_scale=wb_plane[:, cols],
                rhs=hid_codes[:].bitcast(E5M2), rhs_scale=hid_scales[:], start=False, stop=True,
            )

        p0 = sbuf("p0", [P, O], F32)
        nc.vector.tensor_copy(p0[:], p_banks[0][:])
        nc.vector.tensor_copy(pages[0][:].indirect(list7[:]), p0[:])
        nc.sync.dma_start(out[0:P, :], pages[0][:])
        p1 = sbuf("p1", [P, O], F32)
        nc.scalar.copy(p1[:], p_banks[1][:])
        nc.scalar.activation(pages[1][:].indirect(list7[:]), p1[:], ACT.Copy)
        nc.scalar.dma_start(out[P : 2 * P, :], pages[1][:])
